import numpy as np
CORES = [9,10,11,14,17,18,19,22,49,50,51,54]
N = 12
TK = 512
D = 128 * N
EPS = 0.01
def setup_inputs(rng):
    return {"x": (rng.standard_normal((N, 128, TK), dtype=np.float32) * (0.5 + np.abs(rng.standard_normal((1, 1, TK), dtype=np.float32))) + rng.standard_normal((1, 1, TK), dtype=np.float32)), "w": (rng.standard_normal((N, 128, 128), dtype=np.float32) / 11)}
def reference(x, w):
    X = x.astype(np.float64)
    mu = X.sum(axis=(0, 1)) / D
    Z = X - mu
    Z = Z / np.sqrt((Z ** 2).sum(axis=(0, 1)) / D + EPS)
    s = sum(w[r].astype(np.float64).T @ Z[r] for r in range(N)).astype(np.float32)
    return {"y": np.broadcast_to(s, (N,) + s.shape)}

@@ -1,0 +1,208 @@
+from concourse.bass import DstId, RemoteDMATransfer
+from concourse.mybir import AluOpType, ActivationFunctionType
+
+NSIM = 64
+NB = 4
+BW = 128
+PW = 131
+SL = 132
+EPS = 0.01
+
+F = "float32"
+SCRATCH = {
+    "xs": ("sbuf", [128, NB * BW], F), "xq": ("sbuf", [128, NB * BW], F), "wa": ("sbuf", [128, SL], F),
+    "sb": ("sbuf", [128, NB * SL], F),
+    "la": ("sbuf", [128, 4 * SL], F),
+    "lr": ("sbuf", [128, 3 * SL], F),
+    "cs": ("sbuf", [128, 3 * SL], F),
+    "ones": ("sbuf", [128, 128], F), "kd": ("sbuf", [128, 128], F), "ident": ("sbuf", [128, 128], F),
+    "dgs": ("sbuf", [128, 128], F), "dgr": ("sbuf", [128, 128], F),
+    "sm": ("sbuf", [128, 32], F),
+    "tt": ("sbuf", [128, 128], F), "uu": ("sbuf", [128, 128], F), "yo": ("sbuf", [128, 128], F),
+    "yb": ("sbuf", [128, NB * BW], F),
+    "p0": ("psum", [128, 512], F), "p1": ("psum", [128, 512], F), "p2": ("psum", [128, 512], F),
+    "p3": ("psum", [128, 512], F), "pc": ("psum", [128, 512], F), "pt": ("psum", [128, 512], F),
+    "pm": ("psum", [128, 512], F), "pr": ("psum", [128, 512], F),
+}
+SEMAPHORES = (["lw", "m1", "mo", "mk", "me", "idn", "ew", "pcd", "cc", "a1", "sent", "s1", "s2", "ptd"]
+              + ["lx%d" % b for b in range(NB)] + ["sq%d" % b for b in range(NB)] + ["pb%d" % b for b in range(NB)]
+              + ["cb%d" % b for b in range(NB)] + ["y%d" % b for b in range(NB)] + ["st%d" % b for b in range(NB)]
+              + ["r%d" % i for i in range(3)] + ["t%d" % i for i in range(1, 14)])
+
+
+def _bits(m):
+    return bin(m).count("1")
+
+
+def _owners(T, topo, chips, ch):
+    far = [c for c in range(NSIM) if topo.chip(c) in chips and topo.chip(c) != ch]
+    rest = [c for c in range(NSIM) if topo.chip(c) == ch and all(topo.may_write(c, d) for d in far)]
+    rest.sort(key=lambda c: (T.rank_of(c) is not None, c))
+    out = [rest.pop(0)]
+    while rest:
+        other = [c for c in rest if topo.die(c) != topo.die(out[-1])]
+        nxt = other[0] if other else rest[0]
+        rest.remove(nxt)
+        out.append(nxt)
+    return out[:NB]
+
+
+def rank_program(g, core, T, topo):
+    S = T.sem
+    A, ACT = AluOpType, ActivationFunctionType
+    D = 128 * len(T.cores)
+    chips = sorted(set(topo.chip(c) for c in T.cores))
+    ch = topo.chip(core)
+    if ch not in chips:
+        return
+    own = dict((k, _owners(T, topo, chips, k)) for k in chips)
+    rank = T.rank_of(core)
+    mine = own[ch].index(core) if core in own[ch] else None
+    if rank is None and mine is None:
+        return
+    ranks = [c for c in T.cores if topo.chip(c) == ch]
+    pos = chips.index(ch)
+    sent = 0
+
+    def tile(buf, k):
+        return buf[:, k * SL:k * SL + PW]
+
+    def blk(buf, b):
+        return buf[:, b * BW:(b + 1) * BW]
+
+    if rank is not None:
+        g.scalar.dma_start(T.wa[:, 0:128], T.w[:]).then_inc(S.lw, 16)
+        for b in range(NB):
+            q = g.sync if b % 2 == 0 else g.scalar
+            q.dma_start(blk(T.xs, b), blk(T.x, b)).then_inc(S["lx%d" % b], 16)
+        g.vector.memset(T.wa[:, 128:SL], 1.0).then_inc(S.m1, 1)
+    if mine is not None:
+        g.vector.memset(T.ones[:], 1.0).then_inc(S.mo, 1)
+        g.vector.memset(T.sm[:, 0:1], EPS * EPS).then_inc(S.me, 1)
+        g.vector.memset(T.kd[:], 1.0 / D).then_inc(S.mk, 1)
+        g.wait_ge(S.mo, 1)
+        g.affine_select(T.ident[:], T.ones[:], [[-1, 128]], A.is_equal, 0.0, 0, 1).then_inc(S.idn, 1)
+        g.scalar.wait_ge(S.me, 1)
+        g.scalar.activation(T.sm[:, 4:5], T.sm[:, 0:1], ACT.Sqrt).then_inc(S.ew, 1)
+
+    if rank is not None:
+        one = T.wa[:, 128:129]
+        g.tensor.wait_ge(S.lw, 16)
+        g.tensor.wait_ge(S.m1, 1)
+        g.tensor.matmul(T.pc[:, 0:1], T.wa[:, 0:128], one, True, True).then_inc(S.pcd, 1)
+        g.vector.wait_ge(S.pcd, 1)
+        for b in range(NB):
+            g.vector.tensor_copy(T.sb[:, b * SL + 130:b * SL + 131], T.pc[:, 0:1]).then_inc(S.cc, 1)
+        g.wait_ge(S.cc, NB)
+        slot = ranks.index(core)
+        for b in range(NB):
+            p = T["p%d" % b]
+            g.scalar.wait_ge(S["lx%d" % b], 16)
+            g.scalar.activation(blk(T.xq, b), blk(T.xs, b), ACT.Square).then_inc(S["sq%d" % b], 1)
+            g.tensor.wait_ge(S["lx%d" % b], 16)
+            g.tensor.matmul(p[:, 0:129], blk(T.xs, b), T.wa[:, 0:129], True, True).then_inc(S["pb%d" % b], 1)
+            g.tensor.wait_ge(S["sq%d" % b], 1)
+            g.tensor.matmul(p[:, 129:130], blk(T.xq, b), one, True, True).then_inc(S["pb%d" % b], 1)
+            g.vector.wait_ge(S["pb%d" % b], 2)
+            g.vector.tensor_copy(T.sb[:, b * SL:b * SL + 130], p[:, 0:130]).then_inc(S["cb%d" % b], 1)
+            g.wait_ge(S["cb%d" % b], 1)
+            dst = own[ch][b]
+            if dst != core:
+                rid, pid, _ = topo.addr(dst)
+                m = topo.mask(core, dst)
+                g.remote_dma(tile(T.la, slot), tile(T.sb, b), S.a1, S.sent, pid, rid, m)
+                sent += _bits(m)
+
+    if mine is not None:
+        srcs = [tile(T.sb, mine) if c == core else tile(T.la, k) for k, c in enumerate(ranks)]
+        need = sum(_bits(topo.mask(c, core)) for c in ranks if c != core)
+        peers = [own[k][mine] for k in chips if k != ch]
+        g.wait_ge(S.a1, need)
+        m = topo.mask(core, peers[0])
+        for d in peers:
+            m &= topo.mask(core, d)
+        ids = [DstId(rid=topo.addr(d)[0], pnc=topo.addr(d)[1]) for d in peers]
+        g.remote_dma_fused([RemoteDMATransfer(dst_ids=ids, dma_engine_mask=m, remote_sem=S["r%d" % pos], srcs=srcs,
+                                              dsts=[tile(T.lr, pos) for d in peers], alu_op=1)], local_sem=S.sent)
+        sent += _bits(m)
+        v = g.vector
+        v.wait_ge(S.a1, need)
+        if rank is not None:
+            v.wait_ge(S["cb%d" % mine], 1)
+            v.wait_ge(S.cc, NB)
+        v.tensor_tensor(tile(T.cs, 0), srcs[0], srcs[1], A.add).then_inc(S.s1, 1)
+        v.tensor_tensor(tile(T.cs, 1), srcs[2], srcs[3], A.add).then_inc(S.s1, 1)
+        v.wait_ge(S.s1, 2)
+        v.tensor_tensor(tile(T.cs, 2), tile(T.cs, 0), tile(T.cs, 1), A.add).then_inc(S.s2, 1)
+        far = sorted((k for k in chips if k != ch), key=lambda k: (not topo.same_plane(ch, k), k))
+        fa, fb = chips.index(far[0]), chips.index(far[1])
+        na = _bits(topo.mask(own[far[0]][mine], core))
+        nb = _bits(topo.mask(own[far[1]][mine], core))
+        pe = g.tensor
+        pe.wait_ge(S.s2, 1)
+        pe.wait_ge(S.idn, 1)
+        pe.matmul(T.pt[:, 0:128], T.cs[:, 2 * SL:2 * SL + 128], T.ident[:], True, False)
+        pe.wait_ge(S["r%d" % fa], na)
+        pe.matmul(T.pt[:, 0:128], T.lr[:, fa * SL:fa * SL + 128], T.ident[:], False, False)
+        pe.wait_ge(S["r%d" % fb], nb)
+        pe.matmul(T.pt[:, 0:128], T.lr[:, fb * SL:fb * SL + 128], T.ident[:], False, True).then_inc(S.ptd, 1)
+        st1, st = T.sm[:, 12:15], T.sm[:, 8:11]
+        s_, ss_, c_ = T.sm[:, 8:9], T.sm[:, 9:10], T.sm[:, 10:11]
+        m2, u_, sd, rs = T.sm[:, 16:17], T.sm[:, 20:21], T.sm[:, 24:25], T.sm[:, 28:29]
+        a = g.scalar
+        v.wait_ge(S.s2, 1)
+        v.wait_ge(S["r%d" % fa], na)
+        v.tensor_tensor(st1, T.cs[:, 2 * SL + 128:2 * SL + PW], T.lr[:, fa * SL + 128:fa * SL + PW], A.add).then_inc(S.t1, 1)
+        v.wait_ge(S.t1, 1)
+        v.wait_ge(S["r%d" % fb], nb)
+        v.tensor_tensor(st, st1, T.lr[:, fb * SL + 128:fb * SL + PW], A.add).then_inc(S.t2, 1)
+        a.wait_ge(S.t2, 1)
+        a.activation(m2, s_, ACT.Square, scale=1.0 / D).then_inc(S.t3, 1)
+        v.wait_ge(S.t2, 1)
+        v.wait_ge(S.t3, 1)
+        v.tensor_scalar(u_, ss_, 1.0 / D, m2, A.mult, A.subtract).then_inc(S.t4, 1)
+        a.wait_ge(S.t4, 1)
+        a.wait_ge(S.ew, 1)
+        a.activation(sd, u_, ACT.Sqrt, bias=T.sm[:, 4:5]).then_inc(S.t5, 1)
+        a.wait_ge(S.idn, 1)
+        a.activation(T.dgs[:], T.ident[:], ACT.Identity, scale=s_).then_inc(S.t6, 1)
+        v.wait_ge(S.t5, 1)
+        v.reciprocal(rs, sd).then_inc(S.t7, 1)
+        v.wait_ge(S.t7, 1)
+        v.wait_ge(S.idn, 1)
+        v.tensor_scalar(T.dgr[:], T.ident[:], rs, None, A.mult).then_inc(S.t8, 1)
+        pe.wait_ge(S.t6, 1)
+        pe.wait_ge(S.mk, 1)
+        pe.matmul(T.pm[:, 0:128], T.kd[:], T.dgs[:], True, True).then_inc(S.t9, 1)
+        pe.wait_ge(S.t8, 1)
+        pe.wait_ge(S.mo, 1)
+        pe.matmul(T.pr[:, 0:128], T.ones[:], T.dgr[:], True, True).then_inc(S.t10, 1)
+        v.wait_ge(S.t9, 1)
+        v.tensor_scalar(T.tt[:], T.pm[:, 0:128], c_, None, A.mult).then_inc(S.t11, 1)
+        v.wait_ge(S.t11, 1)
+        v.wait_ge(S.ptd, 1)
+        v.tensor_tensor(T.uu[:], T.pt[:, 0:128], T.tt[:], A.subtract).then_inc(S.t12, 1)
+        v.wait_ge(S.t12, 1)
+        v.wait_ge(S.t10, 1)
+        v.tensor_tensor(T.yo[:], T.uu[:], T.pr[:, 0:128], A.mult).then_inc(S.t13, 1)
+        to = [c for c in ranks if c != core]
+        m = topo.mask(core, to[0])
+        for d in to:
+            m &= topo.mask(core, d)
+        ids = [DstId(rid=topo.addr(d)[0], pnc=topo.addr(d)[1]) for d in to]
+        g.wait_ge(S.t13, 1)
+        g.remote_dma_fused([RemoteDMATransfer(dst_ids=ids, dma_engine_mask=m, remote_sem=S["y%d" % mine], srcs=[T.yo[:]],
+                                              dsts=[blk(T.yb, mine) for d in to])], local_sem=S.sent)
+        sent += _bits(m)
+
+    if rank is not None:
+        for b in range(NB):
+            if b == mine:
+                g.sync.wait_ge(S.t13, 1)
+                g.sync.dma_start(blk(T.y, b), T.yo[:]).then_inc(S["st%d" % b], 16)
+            else:
+                g.sync.wait_ge(S["y%d" % b], _bits(topo.mask(own[ch][b], core)))
+                g.sync.dma_start(blk(T.y, b), blk(T.yb, b)).then_inc(S["st%d" % b], 16)
+        for b in range(NB):
+            g.wait_ge(S["st%d" % b], 16)
+    g.wait_ge(S.sent, sent)

@@ -63,6 +63,7 @@ def rank_program(g, core, T, topo):
     ranks = [c for c in T.cores if topo.chip(c) == ch]
     pos = chips.index(ch)
     sent = 0
+    v, pe, a = g.vector, g.tensor, g.scalar
 
     def tile(buf, k):
         return buf[:, k * SL:k * SL + PW]
@@ -70,41 +71,62 @@ def rank_program(g, core, T, topo):
     def blk(buf, b):
         return buf[:, b * BW:(b + 1) * BW]
 
+    def ids(cores):
+        return [DstId(rid=topo.addr(d)[0], pnc=topo.addr(d)[1]) for d in cores]
+
+    def common(cores):
+        m = topo.mask(core, cores[0])
+        for d in cores:
+            m &= topo.mask(core, d)
+        return m
+
     if rank is not None:
-        g.scalar.dma_start(T.wa[:, 0:128], T.w[:]).then_inc(S.lw, 16)
+        a.dma_start(T.wa[:, 0:128], T.w[:]).then_inc(S.lw, 16)
         for b in range(NB):
-            q = g.sync if b % 2 == 0 else g.scalar
+            q = g.sync if b % 2 == 0 else a
             q.dma_start(blk(T.xs, b), blk(T.x, b)).then_inc(S["lx%d" % b], 16)
-        g.vector.memset(T.wa[:, 128:SL], 1.0).then_inc(S.m1, 1)
+        v.memset(T.wa[:, 128:SL], 1.0).then_inc(S.m1, 1)
+    idn = 1
     if mine is not None:
-        g.vector.memset(T.ones[:], 1.0).then_inc(S.mo, 1)
-        g.vector.memset(T.sm[:, 0:1], EPS * EPS).then_inc(S.me, 1)
-        g.vector.memset(T.kd[:], 1.0 / D).then_inc(S.mk, 1)
-        g.wait_ge(S.mo, 1)
-        g.affine_select(T.ident[:], T.ones[:], [[-1, 128]], A.is_equal, 0.0, 0, 1).then_inc(S.idn, 1)
-        g.scalar.wait_ge(S.me, 1)
-        g.scalar.activation(T.sm[:, 4:5], T.sm[:, 0:1], ACT.Sqrt).then_inc(S.ew, 1)
+        maker = own[ch][0] if T.rank_of(own[ch][0]) is None else core
+        v.memset(T.ones[:], 1.0).then_inc(S.mo, 1)
+        v.memset(T.sm[:, 0:1], EPS * EPS).then_inc(S.me, 1)
+        v.memset(T.kd[:], 1.0 / D).then_inc(S.mk, 1)
+        if maker == core:
+            g.wait_ge(S.mo, 1)
+            g.affine_select(T.ident[:], T.ones[:], [[-1, 128]], A.is_equal, 0.0, 0, 1).then_inc(S.idn, 1)
+            if rank is None:
+                to = [c for c in own[ch] if c != core]
+                m = common(to)
+                g.wait_ge(S.idn, 1)
+                g.remote_dma_fused([RemoteDMATransfer(dst_ids=ids(to), dma_engine_mask=m, remote_sem=S.idn,
+                                                      srcs=[T.ident[:]], dsts=[T.ident[:] for d in to])], local_sem=S.sent)
+                sent += _bits(m)
+        else:
+            idn = _bits(topo.mask(maker, core))
+        a.wait_ge(S.me, 1)
+        a.activation(T.sm[:, 4:5], T.sm[:, 0:1], ACT.Sqrt).then_inc(S.ew, 1)
 
     if rank is not None:
         one = T.wa[:, 128:129]
-        g.tensor.wait_ge(S.lw, 16)
-        g.tensor.wait_ge(S.m1, 1)
-        g.tensor.matmul(T.pc[:, 0:1], T.wa[:, 0:128], one, True, True).then_inc(S.pcd, 1)
-        g.vector.wait_ge(S.pcd, 1)
+        pe.wait_ge(S.lw, 16)
+        pe.wait_ge(S.m1, 1)
+        pe.matmul(T.pc[:, 0:1], T.wa[:, 0:128], one, True, True).then_inc(S.pcd, 1)
+        v.wait_ge(S.pcd, 1)
         for b in range(NB):
-            g.vector.tensor_copy(T.sb[:, b * SL + 130:b * SL + 131], T.pc[:, 0:1]).then_inc(S.cc, 1)
+            v.tensor_copy(T.sb[:, b * SL + 130:b * SL + 131], T.pc[:, 0:1]).then_inc(S.cc, 1)
         g.wait_ge(S.cc, NB)
         slot = ranks.index(core)
         for b in range(NB):
             p = T["p%d" % b]
-            g.scalar.wait_ge(S["lx%d" % b], 16)
-            g.scalar.activation(blk(T.xq, b), blk(T.xs, b), ACT.Square).then_inc(S["sq%d" % b], 1)
-            g.tensor.wait_ge(S["lx%d" % b], 16)
-            g.tensor.matmul(p[:, 0:129], blk(T.xs, b), T.wa[:, 0:129], True, True).then_inc(S["pb%d" % b], 1)
-            g.tensor.wait_ge(S["sq%d" % b], 1)
-            g.tensor.matmul(p[:, 129:130], blk(T.xq, b), one, True, True).then_inc(S["pb%d" % b], 1)
-            g.vector.wait_ge(S["pb%d" % b], 2)
-            g.vector.tensor_copy(T.sb[:, b * SL:b * SL + 130], p[:, 0:130]).then_inc(S["cb%d" % b], 1)
+            a.wait_ge(S["lx%d" % b], 16)
+            a.activation(blk(T.xq, b), blk(T.xs, b), ACT.Square).then_inc(S["sq%d" % b], 1)
+            pe.wait_ge(S["lx%d" % b], 16)
+            pe.matmul(p[:, 0:129], blk(T.xs, b), T.wa[:, 0:129], True, True).then_inc(S["pb%d" % b], 1)
+            pe.wait_ge(S["sq%d" % b], 1)
+            pe.matmul(p[:, 129:130], blk(T.xq, b), one, True, True).then_inc(S["pb%d" % b], 1)
+            v.wait_ge(S["pb%d" % b], 2)
+            v.tensor_copy(T.sb[:, b * SL:b * SL + 130], p[:, 0:130]).then_inc(S["cb%d" % b], 1)
             g.wait_ge(S["cb%d" % b], 1)
             dst = own[ch][b]
             if dst != core:
@@ -118,14 +140,10 @@ def rank_program(g, core, T, topo):
         need = sum(_bits(topo.mask(c, core)) for c in ranks if c != core)
         peers = [own[k][mine] for k in chips if k != ch]
         g.wait_ge(S.a1, need)
-        m = topo.mask(core, peers[0])
-        for d in peers:
-            m &= topo.mask(core, d)
-        ids = [DstId(rid=topo.addr(d)[0], pnc=topo.addr(d)[1]) for d in peers]
-        g.remote_dma_fused([RemoteDMATransfer(dst_ids=ids, dma_engine_mask=m, remote_sem=S["r%d" % pos], srcs=srcs,
+        m = common(peers)
+        g.remote_dma_fused([RemoteDMATransfer(dst_ids=ids(peers), dma_engine_mask=m, remote_sem=S["r%d" % pos], srcs=srcs,
                                               dsts=[tile(T.lr, pos) for d in peers], alu_op=1)], local_sem=S.sent)
         sent += _bits(m)
-        v = g.vector
         v.wait_ge(S.a1, need)
         if rank is not None:
             v.wait_ge(S["cb%d" % mine], 1)
@@ -138,9 +156,8 @@ def rank_program(g, core, T, topo):
         fa, fb = chips.index(far[0]), chips.index(far[1])
         na = _bits(topo.mask(own[far[0]][mine], core))
         nb = _bits(topo.mask(own[far[1]][mine], core))
-        pe = g.tensor
         pe.wait_ge(S.s2, 1)
-        pe.wait_ge(S.idn, 1)
+        pe.wait_ge(S.idn, idn)
         pe.matmul(T.pt[:, 0:128], T.cs[:, 2 * SL:2 * SL + 128], T.ident[:], True, False)
         pe.wait_ge(S["r%d" % fa], na)
         pe.matmul(T.pt[:, 0:128], T.lr[:, fa * SL:fa * SL + 128], T.ident[:], False, False)
@@ -149,7 +166,6 @@ def rank_program(g, core, T, topo):
         st1, st = T.sm[:, 12:15], T.sm[:, 8:11]
         s_, ss_, c_ = T.sm[:, 8:9], T.sm[:, 9:10], T.sm[:, 10:11]
         m2, u_, sd, rs = T.sm[:, 16:17], T.sm[:, 20:21], T.sm[:, 24:25], T.sm[:, 28:29]
-        a = g.scalar
         v.wait_ge(S.s2, 1)
         v.wait_ge(S["r%d" % fa], na)
         v.tensor_tensor(st1, T.cs[:, 2 * SL + 128:2 * SL + PW], T.lr[:, fa * SL + 128:fa * SL + PW], A.add).then_inc(S.t1, 1)
@@ -164,12 +180,12 @@ def rank_program(g, core, T, topo):
         a.wait_ge(S.t4, 1)
         a.wait_ge(S.ew, 1)
         a.activation(sd, u_, ACT.Sqrt, bias=T.sm[:, 4:5]).then_inc(S.t5, 1)
-        a.wait_ge(S.idn, 1)
+        a.wait_ge(S.idn, idn)
         a.activation(T.dgs[:], T.ident[:], ACT.Identity, scale=s_).then_inc(S.t6, 1)
         v.wait_ge(S.t5, 1)
         v.reciprocal(rs, sd).then_inc(S.t7, 1)
         v.wait_ge(S.t7, 1)
-        v.wait_ge(S.idn, 1)
+        v.wait_ge(S.idn, idn)
         v.tensor_scalar(T.dgr[:], T.ident[:], rs, None, A.mult).then_inc(S.t8, 1)
         pe.wait_ge(S.t6, 1)
         pe.wait_ge(S.mk, 1)
@@ -186,12 +202,9 @@ def rank_program(g, core, T, topo):
         v.wait_ge(S.t10, 1)
         v.tensor_tensor(T.yo[:], T.uu[:], T.pr[:, 0:128], A.mult).then_inc(S.t13, 1)
         to = [c for c in ranks if c != core]
-        m = topo.mask(core, to[0])
-        for d in to:
-            m &= topo.mask(core, d)
-        ids = [DstId(rid=topo.addr(d)[0], pnc=topo.addr(d)[1]) for d in to]
+        m = common(to)
         g.wait_ge(S.t13, 1)
-        g.remote_dma_fused([RemoteDMATransfer(dst_ids=ids, dma_engine_mask=m, remote_sem=S["y%d" % mine], srcs=[T.yo[:]],
+        g.remote_dma_fused([RemoteDMATransfer(dst_ids=ids(to), dma_engine_mask=m, remote_sem=S["y%d" % mine], srcs=[T.yo[:]],
                                               dsts=[blk(T.yb, mine) for d in to])], local_sem=S.sent)
         sent += _bits(m)
 

from concourse.bass import DstId, RemoteDMATransfer
from concourse.mybir import AluOpType, ActivationFunctionType

NSIM = 64
NB = 4
BW = 128
PW = 131
SL = 132
EPS = 0.01

F = "float32"
SCRATCH = {
    "xs": ("sbuf", [128, NB * BW], F), "xq": ("sbuf", [128, NB * BW], F), "wa": ("sbuf", [128, SL], F),
    "sb": ("sbuf", [128, NB * SL], F),
    "la": ("sbuf", [128, 4 * SL], F),
    "lr": ("sbuf", [128, 3 * SL], F),
    "cs": ("sbuf", [128, 3 * SL], F),
    "ones": ("sbuf", [128, 128], F), "kd": ("sbuf", [128, 128], F), "ident": ("sbuf", [128, 128], F),
    "dgs": ("sbuf", [128, 128], F), "dgr": ("sbuf", [128, 128], F),
    "sm": ("sbuf", [128, 32], F),
    "tt": ("sbuf", [128, 128], F), "uu": ("sbuf", [128, 128], F), "yo": ("sbuf", [128, 128], F),
    "yb": ("sbuf", [128, NB * BW], F),
    "p0": ("psum", [128, 512], F), "p1": ("psum", [128, 512], F), "p2": ("psum", [128, 512], F),
    "p3": ("psum", [128, 512], F), "pc": ("psum", [128, 512], F), "pt": ("psum", [128, 512], F),
    "pm": ("psum", [128, 512], F), "pr": ("psum", [128, 512], F),
}
SEMAPHORES = (["lw", "m1", "mo", "mk", "me", "idn", "ew", "pcd", "cc", "a1", "sent", "s1", "s2", "ptd"]
              + ["lx%d" % b for b in range(NB)] + ["sq%d" % b for b in range(NB)] + ["pb%d" % b for b in range(NB)]
              + ["cb%d" % b for b in range(NB)] + ["y%d" % b for b in range(NB)] + ["st%d" % b for b in range(NB)]
              + ["r%d" % i for i in range(3)] + ["t%d" % i for i in range(1, 14)])


def _bits(m):
    return bin(m).count("1")


def _owners(T, topo, chips, ch):
    far = [c for c in range(NSIM) if topo.chip(c) in chips and topo.chip(c) != ch]
    rest = [c for c in range(NSIM) if topo.chip(c) == ch and all(topo.may_write(c, d) for d in far)]
    rest.sort(key=lambda c: (T.rank_of(c) is not None, c))
    out = [rest.pop(0)]
    while rest:
        other = [c for c in rest if topo.die(c) != topo.die(out[-1])]
        nxt = other[0] if other else rest[0]
        rest.remove(nxt)
        out.append(nxt)
    return out[:NB]


def rank_program(g, core, T, topo):
    S = T.sem
    A, ACT = AluOpType, ActivationFunctionType
    D = 128 * len(T.cores)
    chips = sorted(set(topo.chip(c) for c in T.cores))
    ch = topo.chip(core)
    if ch not in chips:
        return
    own = dict((k, _owners(T, topo, chips, k)) for k in chips)
    rank = T.rank_of(core)
    mine = own[ch].index(core) if core in own[ch] else None
    if rank is None and mine is None:
        return
    ranks = [c for c in T.cores if topo.chip(c) == ch]
    pos = chips.index(ch)
    sent = 0
    v, pe, a = g.vector, g.tensor, g.scalar

    def tile(buf, k):
        return buf[:, k * SL:k * SL + PW]

    def blk(buf, b):
        return buf[:, b * BW:(b + 1) * BW]

    def ids(cores):
        return [DstId(rid=topo.addr(d)[0], pnc=topo.addr(d)[1]) for d in cores]

    def common(cores):
        m = topo.mask(core, cores[0])
        for d in cores:
            m &= topo.mask(core, d)
        return m

    if rank is not None:
        a.dma_start(T.wa[:, 0:128], T.w[:]).then_inc(S.lw, 16)
        for b in range(NB):
            q = g.sync if b % 2 == 0 else a
            q.dma_start(blk(T.xs, b), blk(T.x, b)).then_inc(S["lx%d" % b], 16)
        v.memset(T.wa[:, 128:SL], 1.0).then_inc(S.m1, 1)
    idn = 1
    if mine is not None:
        maker = own[ch][0] if T.rank_of(own[ch][0]) is None else core
        v.memset(T.ones[:], 1.0).then_inc(S.mo, 1)
        v.memset(T.sm[:, 0:1], EPS * EPS).then_inc(S.me, 1)
        v.memset(T.kd[:], 1.0 / D).then_inc(S.mk, 1)
        if maker == core:
            g.wait_ge(S.mo, 1)
            g.affine_select(T.ident[:], T.ones[:], [[-1, 128]], A.is_equal, 0.0, 0, 1).then_inc(S.idn, 1)
            if rank is None:
                to = [c for c in own[ch] if c != core]
                m = common(to)
                g.wait_ge(S.idn, 1)
                g.remote_dma_fused([RemoteDMATransfer(dst_ids=ids(to), dma_engine_mask=m, remote_sem=S.idn,
                                                      srcs=[T.ident[:]], dsts=[T.ident[:] for d in to])], local_sem=S.sent)
                sent += _bits(m)
        else:
            idn = _bits(topo.mask(maker, core))
        a.wait_ge(S.me, 1)
        a.activation(T.sm[:, 4:5], T.sm[:, 0:1], ACT.Sqrt).then_inc(S.ew, 1)

    if rank is not None:
        one = T.wa[:, 128:129]
        pe.wait_ge(S.lw, 16)
        pe.wait_ge(S.m1, 1)
        pe.matmul(T.pc[:, 0:1], T.wa[:, 0:128], one, True, True).then_inc(S.pcd, 1)
        v.wait_ge(S.pcd, 1)
        for b in range(NB):
            v.tensor_copy(T.sb[:, b * SL + 130:b * SL + 131], T.pc[:, 0:1]).then_inc(S.cc, 1)
        g.wait_ge(S.cc, NB)
        slot = ranks.index(core)
        for b in range(NB):
            p = T["p%d" % b]
            a.wait_ge(S["lx%d" % b], 16)
            a.activation(blk(T.xq, b), blk(T.xs, b), ACT.Square).then_inc(S["sq%d" % b], 1)
            pe.wait_ge(S["lx%d" % b], 16)
            pe.matmul(p[:, 0:129], blk(T.xs, b), T.wa[:, 0:129], True, True).then_inc(S["pb%d" % b], 1)
            pe.wait_ge(S["sq%d" % b], 1)
            pe.matmul(p[:, 129:130], blk(T.xq, b), one, True, True).then_inc(S["pb%d" % b], 1)
            v.wait_ge(S["pb%d" % b], 2)
            v.tensor_copy(T.sb[:, b * SL:b * SL + 130], p[:, 0:130]).then_inc(S["cb%d" % b], 1)
            g.wait_ge(S["cb%d" % b], 1)
            dst = own[ch][b]
            if dst != core:
                rid, pid, _ = topo.addr(dst)
                m = topo.mask(core, dst)
                g.remote_dma(tile(T.la, slot), tile(T.sb, b), S.a1, S.sent, pid, rid, m)
                sent += _bits(m)

    if mine is not None:
        srcs = [tile(T.sb, mine) if c == core else tile(T.la, k) for k, c in enumerate(ranks)]
        need = sum(_bits(topo.mask(c, core)) for c in ranks if c != core)
        peers = [own[k][mine] for k in chips if k != ch]
        g.wait_ge(S.a1, need)
        m = common(peers)
        g.remote_dma_fused([RemoteDMATransfer(dst_ids=ids(peers), dma_engine_mask=m, remote_sem=S["r%d" % pos], srcs=srcs,
                                              dsts=[tile(T.lr, pos) for d in peers], alu_op=1)], local_sem=S.sent)
        sent += _bits(m)
        v.wait_ge(S.a1, need)
        if rank is not None:
            v.wait_ge(S["cb%d" % mine], 1)
            v.wait_ge(S.cc, NB)
        v.tensor_tensor(tile(T.cs, 0), srcs[0], srcs[1], A.add).then_inc(S.s1, 1)
        v.tensor_tensor(tile(T.cs, 1), srcs[2], srcs[3], A.add).then_inc(S.s1, 1)
        v.wait_ge(S.s1, 2)
        v.tensor_tensor(tile(T.cs, 2), tile(T.cs, 0), tile(T.cs, 1), A.add).then_inc(S.s2, 1)
        far = sorted((k for k in chips if k != ch), key=lambda k: (not topo.same_plane(ch, k), k))
        fa, fb = chips.index(far[0]), chips.index(far[1])
        na = _bits(topo.mask(own[far[0]][mine], core))
        nb = _bits(topo.mask(own[far[1]][mine], core))
        pe.wait_ge(S.s2, 1)
        pe.wait_ge(S.idn, idn)
        pe.matmul(T.pt[:, 0:128], T.cs[:, 2 * SL:2 * SL + 128], T.ident[:], True, False)
        pe.wait_ge(S["r%d" % fa], na)
        pe.matmul(T.pt[:, 0:128], T.lr[:, fa * SL:fa * SL + 128], T.ident[:], False, False)
        pe.wait_ge(S["r%d" % fb], nb)
        pe.matmul(T.pt[:, 0:128], T.lr[:, fb * SL:fb * SL + 128], T.ident[:], False, True).then_inc(S.ptd, 1)
        st1, st = T.sm[:, 12:15], T.sm[:, 8:11]
        s_, ss_, c_ = T.sm[:, 8:9], T.sm[:, 9:10], T.sm[:, 10:11]
        m2, u_, sd, rs = T.sm[:, 16:17], T.sm[:, 20:21], T.sm[:, 24:25], T.sm[:, 28:29]
        v.wait_ge(S.s2, 1)
        v.wait_ge(S["r%d" % fa], na)
        v.tensor_tensor(st1, T.cs[:, 2 * SL + 128:2 * SL + PW], T.lr[:, fa * SL + 128:fa * SL + PW], A.add).then_inc(S.t1, 1)
        v.wait_ge(S.t1, 1)
        v.wait_ge(S["r%d" % fb], nb)
        v.tensor_tensor(st, st1, T.lr[:, fb * SL + 128:fb * SL + PW], A.add).then_inc(S.t2, 1)
        a.wait_ge(S.t2, 1)
        a.activation(m2, s_, ACT.Square, scale=1.0 / D).then_inc(S.t3, 1)
        v.wait_ge(S.t2, 1)
        v.wait_ge(S.t3, 1)
        v.tensor_scalar(u_, ss_, 1.0 / D, m2, A.mult, A.subtract).then_inc(S.t4, 1)
        a.wait_ge(S.t4, 1)
        a.wait_ge(S.ew, 1)
        a.activation(sd, u_, ACT.Sqrt, bias=T.sm[:, 4:5]).then_inc(S.t5, 1)
        a.wait_ge(S.idn, idn)
        a.activation(T.dgs[:], T.ident[:], ACT.Identity, scale=s_).then_inc(S.t6, 1)
        v.wait_ge(S.t5, 1)
        v.reciprocal(rs, sd).then_inc(S.t7, 1)
        v.wait_ge(S.t7, 1)
        v.wait_ge(S.idn, idn)
        v.tensor_scalar(T.dgr[:], T.ident[:], rs, None, A.mult).then_inc(S.t8, 1)
        pe.wait_ge(S.t6, 1)
        pe.wait_ge(S.mk, 1)
        pe.matmul(T.pm[:, 0:128], T.kd[:], T.dgs[:], True, True).then_inc(S.t9, 1)
        pe.wait_ge(S.t8, 1)
        pe.wait_ge(S.mo, 1)
        pe.matmul(T.pr[:, 0:128], T.ones[:], T.dgr[:], True, True).then_inc(S.t10, 1)
        v.wait_ge(S.t9, 1)
        v.tensor_scalar(T.tt[:], T.pm[:, 0:128], c_, None, A.mult).then_inc(S.t11, 1)
        v.wait_ge(S.t11, 1)
        v.wait_ge(S.ptd, 1)
        v.tensor_tensor(T.uu[:], T.pt[:, 0:128], T.tt[:], A.subtract).then_inc(S.t12, 1)
        v.wait_ge(S.t12, 1)
        v.wait_ge(S.t10, 1)
        v.tensor_tensor(T.yo[:], T.uu[:], T.pr[:, 0:128], A.mult).then_inc(S.t13, 1)
        to = [c for c in ranks if c != core]
        m = common(to)
        g.wait_ge(S.t13, 1)
        g.remote_dma_fused([RemoteDMATransfer(dst_ids=ids(to), dma_engine_mask=m, remote_sem=S["y%d" % mine], srcs=[T.yo[:]],
                                              dsts=[blk(T.yb, mine) for d in to])], local_sem=S.sent)
        sent += _bits(m)

    if rank is not None:
        for b in range(NB):
            if b == mine:
                g.sync.wait_ge(S.t13, 1)
                g.sync.dma_start(blk(T.y, b), T.yo[:]).then_inc(S["st%d" % b], 16)
            else:
                g.sync.wait_ge(S["y%d" % b], _bits(topo.mask(own[ch][b], core)))
                g.sync.dma_start(blk(T.y, b), blk(T.yb, b)).then_inc(S["st%d" % b], 16)
        for b in range(NB):
            g.wait_ge(S["st%d" % b], 16)
    g.wait_ge(S.sent, sent)
